import numpy as np
import ml_dtypes


def mxq(x, axis, fmt="e4m3"):
    dtype, down = {"e4m3": (ml_dtypes.float8_e4m3fn, 7), "e5m2": (ml_dtypes.float8_e5m2, 14)}[fmt]
    v = np.moveaxis(np.asarray(x, np.float32).astype(ml_dtypes.bfloat16).astype(np.float64), axis, -1)
    blocks = v.reshape(v.shape[:-1] + (-1, 32))
    amax = np.abs(blocks).max(-1, keepdims=True)
    byte = np.maximum(np.where(amax > 0, np.frexp(amax)[1] - 1 + 127, 0) - down, 1)
    scale = np.exp2(byte - 127.0)
    codes = (blocks / scale).astype(np.float32).astype(dtype).astype(np.float64)
    return np.moveaxis((codes * scale).reshape(v.shape), -1, axis)


WIDE = False


def mx_kscale(k):
    if not WIDE:
        return np.ones(k)
    levels = np.array([24, -24, 12, -12, 0])
    if k % 512:
        return np.exp2(np.random.permutation(np.resize(levels, k // 32))).repeat(32)
    a = np.empty((k // 512, 16))
    for p in range(k // 512):
        a[p, :8] = np.random.permutation(np.resize(levels, 8))
        for g in range(8):
            far = levels[np.abs(levels - a[p, g]) >= 10]
            a[p, g + 8] = far[np.random.randint(len(far))]
    return np.exp2(a.ravel()).repeat(32)


def f64(x):
    return np.asarray(x).astype(np.float64)


E2M1 = np.array([0.0, 0.5, 1.0, 1.5, 2.0, 3.0, 4.0, 6.0, -0.0, -0.5, -1.0, -1.5, -2.0, -3.0, -4.0, -6.0])


def pack_weight(w, fmt):
    k, n = w.shape
    w = f64(np.asarray(w, np.float32).astype(ml_dtypes.bfloat16)).reshape(k // 32, 32, n)
    amax = np.abs(w).max(1)
    if fmt == "e4m3":
        byte = np.frexp(amax)[1] - 1 + 127 - 7
    else:
        mant, ex = np.frexp(amax / 6.0)
        byte = np.where(mant > 0.5, ex, ex - 1) + 127
    byte = np.clip(np.where(amax > 0, byte, 1), 1, 254)
    scaled = (w * np.exp2(127.0 - byte)[:, None, :]).reshape(k, n).astype(np.float32)
    by_word = np.ascontiguousarray(scaled.reshape(k // 512, 128, 4, n).transpose(0, 1, 3, 2))
    if fmt == "e4m3":
        words = by_word.astype(ml_dtypes.float8_e4m3fn).view(np.uint8)
    else:
        c = by_word.astype(ml_dtypes.float4_e2m1fn).view(np.uint8) & 0xF
        words = (c[..., 0::2] | (c[..., 1::2] << 4)).reshape(k // 512, 128, 2 * n)
    return np.ascontiguousarray(words), np.ascontiguousarray(byte.astype(np.uint8).reshape(k // 512, 16, n))


def unpack_weight(words, scales, fmt):
    g, _, n = scales.shape
    words = np.ascontiguousarray(words).reshape(g, 128, n, -1)
    if fmt == "e4m3":
        vals = words.view(ml_dtypes.float8_e4m3fn).astype(np.float64)
    else:
        nib = np.empty((g, 128, n, 4), np.uint8)
        nib[..., 0::2] = words & 0xF
        nib[..., 1::2] = words >> 4
        vals = E2M1[nib]
    vals = vals * np.repeat(np.exp2(scales.astype(np.float64) - 127.0), 8, axis=1)[..., None]
    return vals.transpose(0, 1, 3, 2).reshape(g * 512, n)


def planes(y):
    n, m = y.shape
    v = y.astype(np.float32).astype(ml_dtypes.bfloat16).astype(np.float64).reshape(n // 32, 32, m)
    top = np.abs(v).max(1)
    byte = np.clip(np.where(top > 0, np.frexp(top)[1] - 1 + 127 - 7, 1), 1, 254)
    codes = (v * np.exp2(127.0 - byte)[:, None, :]).reshape(n, m).astype(np.float32).astype(ml_dtypes.float8_e4m3fn).view(np.uint8)
    words = codes.reshape(n // 512, 128, 4, m).transpose(0, 1, 3, 2)
    return np.ascontiguousarray(words), np.ascontiguousarray(byte.astype(np.uint8).reshape(n // 512, 16, m))


def sigm(f):
    return 1.0 / (1.0 + np.exp(-np.maximum(f, -700.0)))


def gelu(f):
    return 0.5 * f * (1.0 + np.tanh(np.sqrt(2.0 / np.pi) * (f + 0.044715 * f**3)))


K, N, T = 1536, 512, 1536


def setup_inputs():
    n = np.random.standard_normal
    s = mx_kscale(K)[:, None]
    p_wg = pack_weight(n((K, N)) / np.sqrt(K) / s, "e2m1")
    p_wh = pack_weight(n((K, N)) / np.sqrt(K) / s, "e4m3")
    return {
        "x": (n((K, T)) * s).astype(np.float32),
        "wg_words": p_wg[0],
        "wg_scales": p_wg[1],
        "wh_words": p_wh[0],
        "wh_scales": p_wh[1],
        "bg": (0.3 * n(N) - 1.0).astype(np.float32),
        "res": (n((N, T))).astype(np.float32),
    }


def reference(x, wg_words, wg_scales, wh_words, wh_scales, bg, res):
    x_ = mxq(f64(x), 0, "e4m3")
    wg_ = unpack_weight(wg_words, wg_scales, "e2m1")
    wh_ = unpack_weight(wh_words, wh_scales, "e4m3")
    ga = wg_.T @ x_
    gate = sigm(ga + f64(bg)[:, None])
    ha = wh_.T @ x_
    out_0 = f64(res) + gate * (gelu(ha) - f64(res))
    return (out_0,) + planes(out_0)

@@ -1,0 +1,237 @@
+from contextlib import ExitStack
+
+import concourse.mybir as mybir
+
+K, N, T = 1536, 512, 1536
+FLOPS = 2 * 2 * K * N * T
+
+F32 = mybir.dt.float32
+BF16 = mybir.dt.bfloat16
+I32 = mybir.dt.int32
+U8 = mybir.dt.uint8
+FP8X4 = mybir.dt.float8_e4m3fn_x4
+FP4X4 = mybir.dt.float4_e2m1fn_x4
+ACT = mybir.ActivationFunctionType
+ALU = mybir.AluOpType
+
+P = 128
+PACK = 4
+PASSES = K // (P * PACK)
+QUADS = 4
+WH_PLANE = 4
+N_FP4 = 128
+WIDTHS = [128,256,256,256,256,256,128]
+VECTOR_SHARE = 96
+
+
+def interleave(copy, dst, src):
+    copy(
+        out=dst.rearrange("p (c i j) -> p c j i", i=4, j=PACK),
+        in_=src.rearrange("p j (c i) -> p c j i", i=4),
+    )
+
+
+def tile_mix_hway_gelu_pl_kernel(
+    tc, x, wg_words, wg_scales, wh_words, wh_scales, bg, res, out_0, out_1, out_2
+):
+    nc = tc.nc
+    n_tiles = len(WIDTHS)
+    starts = [sum(WIDTHS[:i]) for i in range(n_tiles)]
+    cols = [slice(starts[i], starts[i] + WIDTHS[i]) for i in range(n_tiles)]
+
+    with ExitStack() as ctx:
+        keep = ctx.enter_context(tc.tile_pool(name="keep", bufs=1))
+        work = ctx.enter_context(tc.tile_pool(name="work", bufs=3))
+        psum = ctx.enter_context(tc.psum_pool(name="psum", bufs=2))
+        ctx.enter_context(tc.manual_schedule())
+
+        wg_raw = keep.tile([P, PASSES * 2 * N], U8, align_bytes=64)
+        wh_raw = keep.tile([P, PASSES * N], I32, align_bytes=64)
+        sc_raw = keep.tile([P, PASSES * N], U8, align_bytes=64)
+        wg = keep.tile([P, PACK, PASSES, 2 * P], U8, align_bytes=64)
+        wh = keep.tile([P, PACK, PASSES, P], I32, align_bytes=64)
+        sc = keep.tile([P, PACK, PASSES, P], U8, align_bytes=64)
+        bias = keep.tile([P, PACK], F32)
+        half_bias = keep.tile([P, PACK], F32)
+        zero = keep.tile([P, 1], F32)
+        gelu_bias = keep.tile([P, 1], F32)
+        out_scales = keep.tile([P, T], U8, align_bytes=64)
+
+        nc.vector.memset(sc_raw[:].bitcast(I32), 0)
+        nc.vector.memset(zero[:], 0.0)
+        nc.scalar.activation(out=gelu_bias[:], in_=zero[:], func=ACT.Gelu_apprx_tanh)
+
+        x_raw, res_sb = {}, {}
+
+        def load_x(i, a):
+            x_raw[i, a] = keep.tile([P, PACK, WIDTHS[i]], F32, name="x_raw_%d_%d" % (i, a))
+            rows = x[a * P * PACK : (a + 1) * P * PACK, cols[i]]
+            nc.sync.dma_start(out=x_raw[i, a][:], in_=rows.rearrange("(p j) t -> p j t", j=PACK))
+
+        def load_res(i):
+            res_sb[i] = keep.tile([P, PACK, WIDTHS[i]], F32, name="res_%d" % i)
+            nc.sync.dma_start(out=res_sb[i][:], in_=res[:, cols[i]].rearrange("(p r) t -> p r t", r=PACK))
+
+        def load_scales(scales, first_row):
+            rows = sc_raw[:].bitcast(I32).rearrange("p (a n) -> p a n", a=PASSES)
+            for q in range(QUADS):
+                nc.sync.dma_start(
+                    out=rows[32 * q + first_row : 32 * q + first_row + 4],
+                    in_=scales[:, 4 * q : 4 * q + 4, :].bitcast(I32).rearrange("a r n -> r a n"),
+                )
+
+        nc.sync.dma_start(
+            out=wg_raw[:].bitcast(I32).rearrange("p (a n) -> p a n", a=PASSES),
+            in_=wg_words.bitcast(I32).rearrange("a p n -> p a n"),
+        )
+        load_scales(wg_scales, 0)
+        nc.sync.dma_start(
+            out=wh_raw[:].rearrange("p (a n) -> p a n", a=PASSES),
+            in_=wh_words.rearrange("a p n i -> a p (n i)").bitcast(I32).rearrange("a p n -> p a n"),
+        )
+        load_x(0, 0)
+        load_x(0, 1)
+        load_x(0, 2)
+        load_scales(wh_scales, WH_PLANE)
+        nc.sync.dma_start(out=bias[:], in_=bg.rearrange("(p r) -> p r", r=PACK))
+        for i in range(n_tiles):
+            if i + 1 < n_tiles:
+                load_x(i + 1, 0)
+            load_res(i)
+            if i + 1 < n_tiles:
+                load_x(i + 1, 1)
+                load_x(i + 1, 2)
+
+        nc.vector.tensor_copy(
+            out=wg[:].rearrange("p r a (c i b) -> p (a c) r i b", i=8, b=2),
+            in_=wg_raw[:].rearrange("p (m i r b) -> p m r i b", i=8, r=PACK, b=2),
+        )
+        nc.vector.tensor_copy(
+            out=wh[:].rearrange("p r a (c i) -> p (a c) r i", i=4),
+            in_=wh_raw[:].rearrange("p (m i r) -> p m r i", i=4, r=PACK),
+        )
+        nc.vector.tensor_copy(
+            out=sc[:].rearrange("p r a (c i) -> p (a c) r i", i=16),
+            in_=sc_raw[:].rearrange("p (m i r) -> p m r i", i=16, r=PACK),
+        )
+        nc.vector.tensor_scalar(out=half_bias[:], in0=bias[:], scalar1=0.5, scalar2=None, op0=ALU.mult)
+
+        x_bf, ga, ha, th, val, out_sb, out_bf = {}, {}, {}, {}, {}, {}, {}
+
+        def cast_x(i, a):
+            if not 0 <= i < n_tiles:
+                return
+            w = WIDTHS[i]
+            x_bf[i, a] = work.tile([P, PACK * w], BF16, tag="x_bf", name="x_bf", align_bytes=64)
+            split = w - VECTOR_SHARE if (a == 0 and i >= 2 and w > 128) else w
+            if split < w:
+                interleave(nc.vector.tensor_copy, x_bf[i, a][:, PACK * split :], x_raw[i, a][:, :, split:])
+            interleave(nc.scalar.copy, x_bf[i, a][:, : PACK * split], x_raw[i, a][:, :, :split])
+
+        def multiply(i, a):
+            if not 0 <= i < n_tiles:
+                return
+            w = WIDTHS[i]
+            codes = work.tile([P, w], I32, tag="x_codes", name="x_codes", align_bytes=64)
+            planes = work.tile([P, w], U8, tag="x_scales", name="x_scales", align_bytes=64)
+            nc.vector.quantize_mx(out=codes[:].bitcast(FP8X4), scales=planes[:], in_=x_bf[i, a][:])
+            for u in range(2):
+                if a == 0:
+                    ga[i, u] = psum.tile([P, 2, w], F32, tag="ga%d" % u, name="ga")
+                    ha[i, u] = psum.tile([P, 2, w], F32, tag="ha%d" % u, name="ha")
+                for s in range(2):
+                    r = 2 * u + s
+                    nc.tensor.matmul_mx(
+                        out=ha[i, u][:, s, :],
+                        lhsT=wh[:, r, a, :].bitcast(FP8X4),
+                        lhsT_scale=sc[WH_PLANE:, r, a, :],
+                        rhs=codes[:].bitcast(FP8X4),
+                        rhs_scale=planes[:],
+                        start=(a == 0 and s == 0),
+                        stop=(a == PASSES - 1 and s == 1),
+                    )
+                for s in range(2):
+                    r = 2 * u + s
+                    for c0 in range(0, w, N_FP4):
+                        nc.tensor.matmul_mx(
+                            out=ga[i, u][:, s, c0 : c0 + N_FP4],
+                            lhsT=wg[:, r, a, :].bitcast(FP4X4),
+                            lhsT_scale=sc[:, r, a, :],
+                            rhs=codes[:, c0 : c0 + N_FP4].bitcast(FP8X4),
+                            rhs_scale=planes[:, c0 : c0 + N_FP4],
+                            start=(a == 0 and s == 0 and c0 == 0),
+                            stop=(a == PASSES - 1 and s == 1 and c0 + N_FP4 == w),
+                        )
+
+        def activate(i, u):
+            if not 0 <= i < n_tiles:
+                return
+            w = WIDTHS[i]
+            val[i, u] = work.tile([P, 2, w], F32, tag="val", name="val")
+            th[i, u] = work.tile([P, 2, w], F32, tag="th", name="th")
+            nc.scalar.activation(out=val[i, u][:], in_=ha[i, u][:], func=ACT.Gelu_apprx_tanh, bias=gelu_bias[:])
+            for s in range(2):
+                r = 2 * u + s
+                nc.scalar.activation(
+                    out=th[i, u][:, s, :], in_=ga[i, u][:, s, :], func=ACT.Tanh,
+                    bias=half_bias[:, r : r + 1], scale=0.5,
+                )
+
+        def blend(i, u, step):
+            if not 0 <= i < n_tiles:
+                return
+            carried = res_sb[i][:, 2 * u : 2 * u + 2, :]
+            if step == 0:
+                nc.vector.tensor_tensor(out=val[i, u][:], in0=val[i, u][:], in1=carried, op=ALU.subtract)
+            elif step == 1:
+                nc.vector.scalar_tensor_tensor(
+                    out=val[i, u][:], in0=th[i, u][:], scalar=1.0, in1=val[i, u][:], op0=ALU.add, op1=ALU.mult
+                )
+            else:
+                if u == 0:
+                    out_sb[i] = keep.tile([P, PACK, WIDTHS[i]], F32, name="out_%d" % i)
+                nc.vector.scalar_tensor_tensor(
+                    out=out_sb[i][:, 2 * u : 2 * u + 2, :], in0=val[i, u][:], scalar=0.5, in1=carried,
+                    op0=ALU.mult, op1=ALU.add,
+                )
+                if u == 1:
+                    nc.sync.dma_start(out=out_0[:, cols[i]].rearrange("(p r) t -> p r t", r=PACK), in_=out_sb[i][:])
+
+        def cast_out(i):
+            if not 0 <= i < n_tiles:
+                return
+            out_bf[i] = work.tile([P, PACK * WIDTHS[i]], BF16, tag="out_bf", name="out_bf", align_bytes=64)
+            interleave(nc.vector.tensor_copy, out_bf[i][:], out_sb[i][:])
+
+        def quantize_out(i):
+            if not 0 <= i < n_tiles:
+                return
+            out_codes = keep.tile([P, WIDTHS[i]], I32, name="out_codes_%d" % i, align_bytes=64)
+            nc.vector.quantize_mx(out=out_codes[:].bitcast(FP8X4), scales=out_scales[:, cols[i]], in_=out_bf[i][:])
+            words = out_1[0].rearrange("p t i -> p (t i)").bitcast(I32)
+            nc.sync.dma_start(out=words[:, cols[i]], in_=out_codes[:])
+
+        for i in range(-2, n_tiles + 1):
+            activate(i, 0)
+            blend(i, 0, 0)
+            cast_out(i - 1)
+            cast_x(i + 1, 1)
+            blend(i, 0, 1)
+            multiply(i + 1, 1)
+            cast_x(i + 1, 2)
+            blend(i, 0, 2)
+            multiply(i + 1, 2)
+            quantize_out(i - 1)
+            activate(i, 1)
+            blend(i, 1, 0)
+            cast_x(i + 2, 0)
+            blend(i, 1, 1)
+            multiply(i + 2, 0)
+            blend(i, 1, 2)
+
+        for q in range(QUADS):
+            queue = nc.sync if q % 2 == 0 else nc.scalar
+            queue.dma_start(
+                out=out_2[0].bitcast(I32)[4 * q : 4 * q + 4, :],
+                in_=out_scales[:].bitcast(I32)[32 * q : 32 * q + 4, :],
+            )

@@ -21,13 +21,16 @@ QUADS = 4
 WH_PLANE = 4
 N_FP4 = 128
 WIDTHS = [128,256,256,256,256,256,128]
-VECTOR_SHARE = 96
+VECTOR_SHARE = 160
+RUN = 2
+SCALAR_TAIL = 3
+VECTOR_HEAD = 0
 
 
 def interleave(copy, dst, src):
     copy(
-        out=dst.rearrange("p (c i j) -> p c j i", i=4, j=PACK),
-        in_=src.rearrange("p j (c i) -> p c j i", i=4),
+        out=dst.rearrange("p (c i j) -> p c j i", i=RUN, j=PACK),
+        in_=src.rearrange("p j (c i) -> p c j i", i=RUN),
     )
 
 
@@ -72,27 +75,32 @@ def tile_mix_hway_gelu_pl_kernel(
             res_sb[i] = keep.tile([P, PACK, WIDTHS[i]], F32, name="res_%d" % i)
             nc.sync.dma_start(out=res_sb[i][:], in_=res[:, cols[i]].rearrange("(p r) t -> p r t", r=PACK))
 
-        def load_scales(scales, first_row):
+        def load_scales(scales, first_row, q):
             rows = sc_raw[:].bitcast(I32).rearrange("p (a n) -> p a n", a=PASSES)
-            for q in range(QUADS):
-                nc.sync.dma_start(
-                    out=rows[32 * q + first_row : 32 * q + first_row + 4],
-                    in_=scales[:, 4 * q : 4 * q + 4, :].bitcast(I32).rearrange("a r n -> r a n"),
-                )
+            nc.sync.dma_start(
+                out=rows[32 * q + first_row : 32 * q + first_row + 4],
+                in_=scales[:, 4 * q : 4 * q + 4, :].bitcast(I32).rearrange("a r n -> r a n"),
+            )
 
         nc.sync.dma_start(
             out=wg_raw[:].bitcast(I32).rearrange("p (a n) -> p a n", a=PASSES),
             in_=wg_words.bitcast(I32).rearrange("a p n -> p a n"),
         )
-        load_scales(wg_scales, 0)
+        load_scales(wg_scales, 0, 0)
+        load_scales(wg_scales, 0, 1)
+        load_scales(wg_scales, 0, 2)
+        load_scales(wg_scales, 0, 3)
+        load_scales(wh_scales, WH_PLANE, 0)
         nc.sync.dma_start(
             out=wh_raw[:].rearrange("p (a n) -> p a n", a=PASSES),
             in_=wh_words.rearrange("a p n i -> a p (n i)").bitcast(I32).rearrange("a p n -> p a n"),
         )
         load_x(0, 0)
+        load_scales(wh_scales, WH_PLANE, 1)
+        load_scales(wh_scales, WH_PLANE, 2)
+        load_scales(wh_scales, WH_PLANE, 3)
         load_x(0, 1)
         load_x(0, 2)
-        load_scales(wh_scales, WH_PLANE)
         nc.sync.dma_start(out=bias[:], in_=bg.rearrange("(p r) -> p r", r=PACK))
         for i in range(n_tiles):
             if i + 1 < n_tiles:
@@ -102,21 +110,28 @@ def tile_mix_hway_gelu_pl_kernel(
                 load_x(i + 1, 1)
                 load_x(i + 1, 2)
 
-        nc.vector.tensor_copy(
-            out=wg[:].rearrange("p r a (c i b) -> p (a c) r i b", i=8, b=2),
-            in_=wg_raw[:].rearrange("p (m i r b) -> p m r i b", i=8, r=PACK, b=2),
-        )
-        nc.vector.tensor_copy(
-            out=wh[:].rearrange("p r a (c i) -> p (a c) r i", i=4),
-            in_=wh_raw[:].rearrange("p (m i r) -> p m r i", i=4, r=PACK),
-        )
-        nc.vector.tensor_copy(
-            out=sc[:].rearrange("p r a (c i) -> p (a c) r i", i=16),
-            in_=sc_raw[:].rearrange("p (m i r) -> p m r i", i=16, r=PACK),
-        )
-        nc.vector.tensor_scalar(out=half_bias[:], in0=bias[:], scalar1=0.5, scalar2=None, op0=ALU.mult)
+        def deal_wg(u):
+            pair = slice(2 * u, 2 * u + 2)
+            nc.vector.tensor_copy(
+                out=wg[:, pair].rearrange("p r a (c i b) -> p (a c) r i b", i=8, b=2),
+                in_=wg_raw[:].rearrange("p (m i r b) -> p m r i b", i=8, r=PACK, b=2)[:, :, pair],
+            )
 
-        x_bf, ga, ha, th, val, out_sb, out_bf = {}, {}, {}, {}, {}, {}, {}
+        def deal_sc(u):
+            pair = slice(2 * u, 2 * u + 2)
+            nc.vector.tensor_copy(
+                out=sc[:, pair].rearrange("p r a (c i) -> p (a c) r i", i=16),
+                in_=sc_raw[:].rearrange("p (m i r) -> p m r i", i=16, r=PACK)[:, :, pair],
+            )
+
+        def deal_wh(u):
+            pair = slice(2 * u, 2 * u + 2)
+            nc.vector.tensor_copy(
+                out=wh[:, pair].rearrange("p r a (c i) -> p (a c) i r", i=4),
+                in_=wh_raw[:].rearrange("p (m i r) -> p m i r", i=4, r=PACK)[:, :, :, pair],
+            )
+
+        x_bf, codes, planes, ga, ha, th, val, out_sb, out_bf = {}, {}, {}, {}, {}, {}, {}, {}, {}
 
         def cast_x(i, a):
             if not 0 <= i < n_tiles:
@@ -124,44 +139,54 @@ def tile_mix_hway_gelu_pl_kernel(
             w = WIDTHS[i]
             x_bf[i, a] = work.tile([P, PACK * w], BF16, tag="x_bf", name="x_bf", align_bytes=64)
             split = w - VECTOR_SHARE if (a == 0 and i >= 2 and w > 128) else w
+            if (i, a) in []:
+                split = 0
             if split < w:
                 interleave(nc.vector.tensor_copy, x_bf[i, a][:, PACK * split :], x_raw[i, a][:, :, split:])
-            interleave(nc.scalar.copy, x_bf[i, a][:, : PACK * split], x_raw[i, a][:, :, :split])
+            if split > 0:
+                interleave(nc.scalar.copy, x_bf[i, a][:, : PACK * split], x_raw[i, a][:, :, :split])
+
+        def quantize_x(i, a):
+            w = WIDTHS[i]
+            codes[i, a] = work.tile([P, w], I32, tag="x_codes", name="x_codes", align_bytes=64, bufs=4)
+            planes[i, a] = work.tile([P, w], U8, tag="x_scales", name="x_scales", align_bytes=64, bufs=4)
+            nc.vector.quantize_mx(out=codes[i, a][:].bitcast(FP8X4), scales=planes[i, a][:], in_=x_bf[i, a][:])
+
+        def matmuls(i, a, u):
+            w = WIDTHS[i]
+            if a == 0:
+                ga[i, u] = psum.tile([P, 2, w], F32, tag="ga%d" % u, name="ga")
+                ha[i, u] = psum.tile([P, 2, w], F32, tag="ha%d" % u, name="ha")
+            for s in range(2):
+                r = 2 * u + s
+                nc.tensor.matmul_mx(
+                    out=ha[i, u][:, s, :],
+                    lhsT=wh[:, r, a, :].bitcast(FP8X4),
+                    lhsT_scale=sc[WH_PLANE:, r, a, :],
+                    rhs=codes[i, a][:].bitcast(FP8X4),
+                    rhs_scale=planes[i, a][:],
+                    start=(a == 0 and s == 0),
+                    stop=(a == PASSES - 1 and s == 1),
+                )
+            for s in range(2):
+                r = 2 * u + s
+                for c0 in range(0, w, N_FP4):
+                    nc.tensor.matmul_mx(
+                        out=ga[i, u][:, s, c0 : c0 + N_FP4],
+                        lhsT=wg[:, r, a, :].bitcast(FP4X4),
+                        lhsT_scale=sc[:, r, a, :],
+                        rhs=codes[i, a][:, c0 : c0 + N_FP4].bitcast(FP8X4),
+                        rhs_scale=planes[i, a][:, c0 : c0 + N_FP4],
+                        start=(a == 0 and s == 0 and c0 == 0),
+                        stop=(a == PASSES - 1 and s == 1 and c0 + N_FP4 == w),
+                    )
 
         def multiply(i, a):
             if not 0 <= i < n_tiles:
                 return
-            w = WIDTHS[i]
-            codes = work.tile([P, w], I32, tag="x_codes", name="x_codes", align_bytes=64)
-            planes = work.tile([P, w], U8, tag="x_scales", name="x_scales", align_bytes=64)
-            nc.vector.quantize_mx(out=codes[:].bitcast(FP8X4), scales=planes[:], in_=x_bf[i, a][:])
+            quantize_x(i, a)
             for u in range(2):
-                if a == 0:
-                    ga[i, u] = psum.tile([P, 2, w], F32, tag="ga%d" % u, name="ga")
-                    ha[i, u] = psum.tile([P, 2, w], F32, tag="ha%d" % u, name="ha")
-                for s in range(2):
-                    r = 2 * u + s
-                    nc.tensor.matmul_mx(
-                        out=ha[i, u][:, s, :],
-                        lhsT=wh[:, r, a, :].bitcast(FP8X4),
-                        lhsT_scale=sc[WH_PLANE:, r, a, :],
-                        rhs=codes[:].bitcast(FP8X4),
-                        rhs_scale=planes[:],
-                        start=(a == 0 and s == 0),
-                        stop=(a == PASSES - 1 and s == 1),
-                    )
-                for s in range(2):
-                    r = 2 * u + s
-                    for c0 in range(0, w, N_FP4):
-                        nc.tensor.matmul_mx(
-                            out=ga[i, u][:, s, c0 : c0 + N_FP4],
-                            lhsT=wg[:, r, a, :].bitcast(FP4X4),
-                            lhsT_scale=sc[:, r, a, :],
-                            rhs=codes[:, c0 : c0 + N_FP4].bitcast(FP8X4),
-                            rhs_scale=planes[:, c0 : c0 + N_FP4],
-                            start=(a == 0 and s == 0 and c0 == 0),
-                            stop=(a == PASSES - 1 and s == 1 and c0 + N_FP4 == w),
-                        )
+                matmuls(i, a, u)
 
         def activate(i, u):
             if not 0 <= i < n_tiles:
@@ -201,7 +226,8 @@ def tile_mix_hway_gelu_pl_kernel(
             if not 0 <= i < n_tiles:
                 return
             out_bf[i] = work.tile([P, PACK * WIDTHS[i]], BF16, tag="out_bf", name="out_bf", align_bytes=64)
-            interleave(nc.vector.tensor_copy, out_bf[i][:], out_sb[i][:])
+            copy = nc.scalar.copy if n_tiles - SCALAR_TAIL <= i < n_tiles - 1 else nc.vector.tensor_copy
+            interleave(copy, out_bf[i][:], out_sb[i][:])
 
         def quantize_out(i):
             if not 0 <= i < n_tiles:
@@ -211,23 +237,55 @@ def tile_mix_hway_gelu_pl_kernel(
             words = out_1[0].rearrange("p t i -> p (t i)").bitcast(I32)
             nc.sync.dma_start(out=words[:, cols[i]], in_=out_codes[:])
 
-        for i in range(-2, n_tiles + 1):
+        deal_wg(0)
+        deal_wg(1)
+        deal_wh(0)
+        deal_sc(0)
+        for a in range(PASSES):
+            cast_x(0, a)
+            quantize_x(0, a)
+            matmuls(0, a, 0)
+        nc.vector.tensor_scalar(out=half_bias[:], in0=bias[:], scalar1=0.5, scalar2=None, op0=ALU.mult)
+        deal_wh(1)
+        deal_sc(1)
+        for a in range(PASSES):
+            matmuls(0, a, 1)
+        cast_x(1, 0)
+        multiply(1, 0)
+        late = n_tiles - SCALAR_TAIL
+        for i in range(n_tiles - 1):
             activate(i, 0)
             blend(i, 0, 0)
-            cast_out(i - 1)
+            if i - 1 < late:
+                cast_out(i - 1)
             cast_x(i + 1, 1)
             blend(i, 0, 1)
             multiply(i + 1, 1)
             cast_x(i + 1, 2)
             blend(i, 0, 2)
             multiply(i + 1, 2)
-            quantize_out(i - 1)
+            if i - 1 < late:
+                quantize_out(i - 1)
             activate(i, 1)
             blend(i, 1, 0)
             cast_x(i + 2, 0)
+            if i - 1 >= late:
+                cast_out(i - 1)
             blend(i, 1, 1)
             multiply(i + 2, 0)
+            if i - 1 >= late:
+                quantize_out(i - 1)
             blend(i, 1, 2)
+        last = n_tiles - 1
+        activate(last, 0)
+        activate(last, 1)
+        cast_out(last - 1)
+        for step in range(3):
+            blend(last, 0, step)
+            blend(last, 1, step)
+        quantize_out(last - 1)
+        cast_out(last)
+        quantize_out(last)
 
         for q in range(QUADS):
             queue = nc.sync if q % 2 == 0 else nc.scalar

@@ -21,10 +21,25 @@ QUADS = 4
 WH_PLANE = 4
 N_FP4 = 128
 WIDTHS = [128,256,256,256,256,256,128]
+X_GROUPS = [1,1,1,1,1,1,1]
+RES_GROUPS = [1,1,1,1,1,2]
+OUT_GROUPS = [3,2,1,1]
+WORD_GROUPS = [5,2]
 VECTOR_SHARE = 160
 RUN = 2
 SCALAR_TAIL = 3
 VECTOR_HEAD = 0
+
+
+def spans(groups):
+    result = []
+    first = 0
+    for size in groups:
+        lo, hi = sum(WIDTHS[:first]), sum(WIDTHS[: first + size])
+        for i in range(first, first + size):
+            result.append((first, first + size - 1, slice(lo, hi), slice(sum(WIDTHS[:i]) - lo, sum(WIDTHS[: i + 1]) - lo)))
+        first = first + size
+    return result
 
 
 def interleave(copy, dst, src):
@@ -64,16 +79,27 @@ def tile_mix_hway_gelu_pl_kernel(
         nc.vector.memset(zero[:], 0.0)
         nc.scalar.activation(out=gelu_bias[:], in_=zero[:], func=ACT.Gelu_apprx_tanh)
 
-        x_raw, res_sb = {}, {}
+        x_raw, res_sb, out_sb, out_codes = {}, {}, {}, {}
+        x_span, res_span, out_span, word_span = spans(X_GROUPS), spans(RES_GROUPS), spans(OUT_GROUPS), spans(WORD_GROUPS)
 
         def load_x(i, a):
-            x_raw[i, a] = keep.tile([P, PACK, WIDTHS[i]], F32, name="x_raw_%d_%d" % (i, a))
-            rows = x[a * P * PACK : (a + 1) * P * PACK, cols[i]]
-            nc.sync.dma_start(out=x_raw[i, a][:], in_=rows.rearrange("(p j) t -> p j t", j=PACK))
+            first, last, wide, part = x_span[i]
+            if i != first:
+                return
+            raw = keep.tile([P, PACK, wide.stop - wide.start], F32, name="x_raw_%d_%d" % (i, a))
+            rows = x[a * P * PACK : (a + 1) * P * PACK, wide]
+            nc.sync.dma_start(out=raw[:], in_=rows.rearrange("(p j) t -> p j t", j=PACK))
+            for m in range(first, last + 1):
+                x_raw[m, a] = raw[:, :, x_span[m][3]]
 
         def load_res(i):
-            res_sb[i] = keep.tile([P, PACK, WIDTHS[i]], F32, name="res_%d" % i)
-            nc.sync.dma_start(out=res_sb[i][:], in_=res[:, cols[i]].rearrange("(p r) t -> p r t", r=PACK))
+            first, last, wide, part = res_span[i]
+            if i != first:
+                return
+            raw = keep.tile([P, PACK, wide.stop - wide.start], F32, name="res_%d" % i)
+            nc.sync.dma_start(out=raw[:], in_=res[:, wide].rearrange("(p r) t -> p r t", r=PACK))
+            for m in range(first, last + 1):
+                res_sb[m] = raw[:, :, res_span[m][3]]
 
         def load_scales(scales, first_row, q):
             rows = sc_raw[:].bitcast(I32).rearrange("p (a n) -> p a n", a=PASSES)
@@ -131,7 +157,7 @@ def tile_mix_hway_gelu_pl_kernel(
                 in_=wh_raw[:].rearrange("p (m i r) -> p m i r", i=4, r=PACK)[:, :, :, pair],
             )
 
-        x_bf, codes, planes, ga, ha, th, val, out_sb, out_bf = {}, {}, {}, {}, {}, {}, {}, {}, {}
+        x_bf, codes, planes, ga, ha, th, val, out_bf, out_wide, words_wide = {}, {}, {}, {}, {}, {}, {}, {}, {}, {}
 
         def cast_x(i, a):
             if not 0 <= i < n_tiles:
@@ -213,29 +239,36 @@ def tile_mix_hway_gelu_pl_kernel(
                     out=val[i, u][:], in0=th[i, u][:], scalar=1.0, in1=val[i, u][:], op0=ALU.add, op1=ALU.mult
                 )
             else:
-                if u == 0:
-                    out_sb[i] = keep.tile([P, PACK, WIDTHS[i]], F32, name="out_%d" % i)
+                first, last, wide, part = out_span[i]
+                if u == 0 and i == first:
+                    out_wide[first] = keep.tile([P, PACK, wide.stop - wide.start], F32, name="out_%d" % i)
+                out_sb[i] = out_wide[first][:, :, part]
                 nc.vector.scalar_tensor_tensor(
                     out=out_sb[i][:, 2 * u : 2 * u + 2, :], in0=val[i, u][:], scalar=0.5, in1=carried,
                     op0=ALU.mult, op1=ALU.add,
                 )
-                if u == 1:
-                    nc.sync.dma_start(out=out_0[:, cols[i]].rearrange("(p r) t -> p r t", r=PACK), in_=out_sb[i][:])
+                if u == 1 and i == last:
+                    nc.sync.dma_start(out=out_0[:, wide].rearrange("(p r) t -> p r t", r=PACK), in_=out_wide[first][:])
 
         def cast_out(i):
             if not 0 <= i < n_tiles:
                 return
             out_bf[i] = work.tile([P, PACK * WIDTHS[i]], BF16, tag="out_bf", name="out_bf", align_bytes=64)
             copy = nc.scalar.copy if n_tiles - SCALAR_TAIL <= i < n_tiles - 1 else nc.vector.tensor_copy
-            interleave(copy, out_bf[i][:], out_sb[i][:])
+            interleave(copy, out_bf[i][:], out_sb[i])
 
         def quantize_out(i):
             if not 0 <= i < n_tiles:
                 return
-            out_codes = keep.tile([P, WIDTHS[i]], I32, name="out_codes_%d" % i, align_bytes=64)
-            nc.vector.quantize_mx(out=out_codes[:].bitcast(FP8X4), scales=out_scales[:, cols[i]], in_=out_bf[i][:])
-            words = out_1[0].rearrange("p t i -> p (t i)").bitcast(I32)
-            nc.sync.dma_start(out=words[:, cols[i]], in_=out_codes[:])
+            first, last, wide, part = word_span[i]
+            if i == first:
+                words_wide[first] = keep.tile([P, wide.stop - wide.start], I32, name="out_codes_%d" % i, align_bytes=64)
+            nc.vector.quantize_mx(
+                out=words_wide[first][:, part].bitcast(FP8X4), scales=out_scales[:, cols[i]], in_=out_bf[i][:]
+            )
+            if i == last:
+                words = out_1[0].rearrange("p t i -> p (t i)").bitcast(I32)
+                nc.sync.dma_start(out=words[:, wide], in_=words_wide[first][:])
 
         deal_wg(0)
         deal_wg(1)

from contextlib import ExitStack

import concourse.mybir as mybir

K, N, T = 1536, 512, 1536
FLOPS = 2 * 2 * K * N * T

F32 = mybir.dt.float32
BF16 = mybir.dt.bfloat16
I32 = mybir.dt.int32
U8 = mybir.dt.uint8
FP8X4 = mybir.dt.float8_e4m3fn_x4
FP4X4 = mybir.dt.float4_e2m1fn_x4
ACT = mybir.ActivationFunctionType
ALU = mybir.AluOpType

P = 128
PACK = 4
PASSES = K // (P * PACK)
QUADS = 4
WH_PLANE = 4
N_FP4 = 128
WIDTHS = [128,256,256,256,256,256,128]
X_GROUPS = [1,1,1,1,1,1,1]
RES_GROUPS = [1,1,1,1,1,2]
OUT_GROUPS = [3,2,1,1]
WORD_GROUPS = [5,2]
VECTOR_SHARE = 160
RUN = 2
SCALAR_TAIL = 3
VECTOR_HEAD = 0


def spans(groups):
    result = []
    first = 0
    for size in groups:
        lo, hi = sum(WIDTHS[:first]), sum(WIDTHS[: first + size])
        for i in range(first, first + size):
            result.append((first, first + size - 1, slice(lo, hi), slice(sum(WIDTHS[:i]) - lo, sum(WIDTHS[: i + 1]) - lo)))
        first = first + size
    return result


def interleave(copy, dst, src):
    copy(
        out=dst.rearrange("p (c i j) -> p c j i", i=RUN, j=PACK),
        in_=src.rearrange("p j (c i) -> p c j i", i=RUN),
    )


def tile_mix_hway_gelu_pl_kernel(
    tc, x, wg_words, wg_scales, wh_words, wh_scales, bg, res, out_0, out_1, out_2
):
    nc = tc.nc
    n_tiles = len(WIDTHS)
    starts = [sum(WIDTHS[:i]) for i in range(n_tiles)]
    cols = [slice(starts[i], starts[i] + WIDTHS[i]) for i in range(n_tiles)]

    with ExitStack() as ctx:
        keep = ctx.enter_context(tc.tile_pool(name="keep", bufs=1))
        work = ctx.enter_context(tc.tile_pool(name="work", bufs=3))
        psum = ctx.enter_context(tc.psum_pool(name="psum", bufs=2))
        ctx.enter_context(tc.manual_schedule())

        wg_raw = keep.tile([P, PASSES * 2 * N], U8, align_bytes=64)
        wh_raw = keep.tile([P, PASSES * N], I32, align_bytes=64)
        sc_raw = keep.tile([P, PASSES * N], U8, align_bytes=64)
        wg = keep.tile([P, PACK, PASSES, 2 * P], U8, align_bytes=64)
        wh = keep.tile([P, PACK, PASSES, P], I32, align_bytes=64)
        sc = keep.tile([P, PACK, PASSES, P], U8, align_bytes=64)
        bias = keep.tile([P, PACK], F32)
        half_bias = keep.tile([P, PACK], F32)
        zero = keep.tile([P, 1], F32)
        gelu_bias = keep.tile([P, 1], F32)
        out_scales = keep.tile([P, T], U8, align_bytes=64)

        nc.vector.memset(sc_raw[:].bitcast(I32), 0)
        nc.vector.memset(zero[:], 0.0)
        nc.scalar.activation(out=gelu_bias[:], in_=zero[:], func=ACT.Gelu_apprx_tanh)

        x_raw, res_sb, out_sb, out_codes = {}, {}, {}, {}
        x_span, res_span, out_span, word_span = spans(X_GROUPS), spans(RES_GROUPS), spans(OUT_GROUPS), spans(WORD_GROUPS)

        def load_x(i, a):
            first, last, wide, part = x_span[i]
            if i != first:
                return
            raw = keep.tile([P, PACK, wide.stop - wide.start], F32, name="x_raw_%d_%d" % (i, a))
            rows = x[a * P * PACK : (a + 1) * P * PACK, wide]
            nc.sync.dma_start(out=raw[:], in_=rows.rearrange("(p j) t -> p j t", j=PACK))
            for m in range(first, last + 1):
                x_raw[m, a] = raw[:, :, x_span[m][3]]

        def load_res(i):
            first, last, wide, part = res_span[i]
            if i != first:
                return
            raw = keep.tile([P, PACK, wide.stop - wide.start], F32, name="res_%d" % i)
            nc.sync.dma_start(out=raw[:], in_=res[:, wide].rearrange("(p r) t -> p r t", r=PACK))
            for m in range(first, last + 1):
                res_sb[m] = raw[:, :, res_span[m][3]]

        def load_scales(scales, first_row, q):
            rows = sc_raw[:].bitcast(I32).rearrange("p (a n) -> p a n", a=PASSES)
            nc.sync.dma_start(
                out=rows[32 * q + first_row : 32 * q + first_row + 4],
                in_=scales[:, 4 * q : 4 * q + 4, :].bitcast(I32).rearrange("a r n -> r a n"),
            )

        nc.sync.dma_start(
            out=wg_raw[:].bitcast(I32).rearrange("p (a n) -> p a n", a=PASSES),
            in_=wg_words.bitcast(I32).rearrange("a p n -> p a n"),
        )
        load_scales(wg_scales, 0, 0)
        load_scales(wg_scales, 0, 1)
        load_scales(wg_scales, 0, 2)
        load_scales(wg_scales, 0, 3)
        load_scales(wh_scales, WH_PLANE, 0)
        nc.sync.dma_start(
            out=wh_raw[:].rearrange("p (a n) -> p a n", a=PASSES),
            in_=wh_words.rearrange("a p n i -> a p (n i)").bitcast(I32).rearrange("a p n -> p a n"),
        )
        load_x(0, 0)
        load_scales(wh_scales, WH_PLANE, 1)
        load_scales(wh_scales, WH_PLANE, 2)
        load_scales(wh_scales, WH_PLANE, 3)
        load_x(0, 1)
        load_x(0, 2)
        nc.sync.dma_start(out=bias[:], in_=bg.rearrange("(p r) -> p r", r=PACK))
        for i in range(n_tiles):
            if i + 1 < n_tiles:
                load_x(i + 1, 0)
            load_res(i)
            if i + 1 < n_tiles:
                load_x(i + 1, 1)
                load_x(i + 1, 2)

        def deal_wg(u):
            pair = slice(2 * u, 2 * u + 2)
            nc.vector.tensor_copy(
                out=wg[:, pair].rearrange("p r a (c i b) -> p (a c) r i b", i=8, b=2),
                in_=wg_raw[:].rearrange("p (m i r b) -> p m r i b", i=8, r=PACK, b=2)[:, :, pair],
            )

        def deal_sc(u):
            pair = slice(2 * u, 2 * u + 2)
            nc.vector.tensor_copy(
                out=sc[:, pair].rearrange("p r a (c i) -> p (a c) r i", i=16),
                in_=sc_raw[:].rearrange("p (m i r) -> p m r i", i=16, r=PACK)[:, :, pair],
            )

        def deal_wh(u):
            pair = slice(2 * u, 2 * u + 2)
            nc.vector.tensor_copy(
                out=wh[:, pair].rearrange("p r a (c i) -> p (a c) i r", i=4),
                in_=wh_raw[:].rearrange("p (m i r) -> p m i r", i=4, r=PACK)[:, :, :, pair],
            )

        x_bf, codes, planes, ga, ha, th, val, out_bf, out_wide, words_wide = {}, {}, {}, {}, {}, {}, {}, {}, {}, {}

        def cast_x(i, a):
            if not 0 <= i < n_tiles:
                return
            w = WIDTHS[i]
            x_bf[i, a] = work.tile([P, PACK * w], BF16, tag="x_bf", name="x_bf", align_bytes=64)
            split = w - VECTOR_SHARE if (a == 0 and i >= 2 and w > 128) else w
            if (i, a) in []:
                split = 0
            if split < w:
                interleave(nc.vector.tensor_copy, x_bf[i, a][:, PACK * split :], x_raw[i, a][:, :, split:])
            if split > 0:
                interleave(nc.scalar.copy, x_bf[i, a][:, : PACK * split], x_raw[i, a][:, :, :split])

        def quantize_x(i, a):
            w = WIDTHS[i]
            codes[i, a] = work.tile([P, w], I32, tag="x_codes", name="x_codes", align_bytes=64, bufs=4)
            planes[i, a] = work.tile([P, w], U8, tag="x_scales", name="x_scales", align_bytes=64, bufs=4)
            nc.vector.quantize_mx(out=codes[i, a][:].bitcast(FP8X4), scales=planes[i, a][:], in_=x_bf[i, a][:])

        def matmuls(i, a, u):
            w = WIDTHS[i]
            if a == 0:
                ga[i, u] = psum.tile([P, 2, w], F32, tag="ga%d" % u, name="ga")
                ha[i, u] = psum.tile([P, 2, w], F32, tag="ha%d" % u, name="ha")
            for s in range(2):
                r = 2 * u + s
                nc.tensor.matmul_mx(
                    out=ha[i, u][:, s, :],
                    lhsT=wh[:, r, a, :].bitcast(FP8X4),
                    lhsT_scale=sc[WH_PLANE:, r, a, :],
                    rhs=codes[i, a][:].bitcast(FP8X4),
                    rhs_scale=planes[i, a][:],
                    start=(a == 0 and s == 0),
                    stop=(a == PASSES - 1 and s == 1),
                )
            for s in range(2):
                r = 2 * u + s
                for c0 in range(0, w, N_FP4):
                    nc.tensor.matmul_mx(
                        out=ga[i, u][:, s, c0 : c0 + N_FP4],
                        lhsT=wg[:, r, a, :].bitcast(FP4X4),
                        lhsT_scale=sc[:, r, a, :],
                        rhs=codes[i, a][:, c0 : c0 + N_FP4].bitcast(FP8X4),
                        rhs_scale=planes[i, a][:, c0 : c0 + N_FP4],
                        start=(a == 0 and s == 0 and c0 == 0),
                        stop=(a == PASSES - 1 and s == 1 and c0 + N_FP4 == w),
                    )

        def multiply(i, a):
            if not 0 <= i < n_tiles:
                return
            quantize_x(i, a)
            for u in range(2):
                matmuls(i, a, u)

        def activate(i, u):
            if not 0 <= i < n_tiles:
                return
            w = WIDTHS[i]
            val[i, u] = work.tile([P, 2, w], F32, tag="val", name="val")
            th[i, u] = work.tile([P, 2, w], F32, tag="th", name="th")
            nc.scalar.activation(out=val[i, u][:], in_=ha[i, u][:], func=ACT.Gelu_apprx_tanh, bias=gelu_bias[:])
            for s in range(2):
                r = 2 * u + s
                nc.scalar.activation(
                    out=th[i, u][:, s, :], in_=ga[i, u][:, s, :], func=ACT.Tanh,
                    bias=half_bias[:, r : r + 1], scale=0.5,
                )

        def blend(i, u, step):
            if not 0 <= i < n_tiles:
                return
            carried = res_sb[i][:, 2 * u : 2 * u + 2, :]
            if step == 0:
                nc.vector.tensor_tensor(out=val[i, u][:], in0=val[i, u][:], in1=carried, op=ALU.subtract)
            elif step == 1:
                nc.vector.scalar_tensor_tensor(
                    out=val[i, u][:], in0=th[i, u][:], scalar=1.0, in1=val[i, u][:], op0=ALU.add, op1=ALU.mult
                )
            else:
                first, last, wide, part = out_span[i]
                if u == 0 and i == first:
                    out_wide[first] = keep.tile([P, PACK, wide.stop - wide.start], F32, name="out_%d" % i)
                out_sb[i] = out_wide[first][:, :, part]
                nc.vector.scalar_tensor_tensor(
                    out=out_sb[i][:, 2 * u : 2 * u + 2, :], in0=val[i, u][:], scalar=0.5, in1=carried,
                    op0=ALU.mult, op1=ALU.add,
                )
                if u == 1 and i == last:
                    nc.sync.dma_start(out=out_0[:, wide].rearrange("(p r) t -> p r t", r=PACK), in_=out_wide[first][:])

        def cast_out(i):
            if not 0 <= i < n_tiles:
                return
            out_bf[i] = work.tile([P, PACK * WIDTHS[i]], BF16, tag="out_bf", name="out_bf", align_bytes=64)
            copy = nc.scalar.copy if n_tiles - SCALAR_TAIL <= i < n_tiles - 1 else nc.vector.tensor_copy
            interleave(copy, out_bf[i][:], out_sb[i])

        def quantize_out(i):
            if not 0 <= i < n_tiles:
                return
            first, last, wide, part = word_span[i]
            if i == first:
                words_wide[first] = keep.tile([P, wide.stop - wide.start], I32, name="out_codes_%d" % i, align_bytes=64)
            nc.vector.quantize_mx(
                out=words_wide[first][:, part].bitcast(FP8X4), scales=out_scales[:, cols[i]], in_=out_bf[i][:]
            )
            if i == last:
                words = out_1[0].rearrange("p t i -> p (t i)").bitcast(I32)
                nc.sync.dma_start(out=words[:, wide], in_=words_wide[first][:])

        deal_wg(0)
        deal_wg(1)
        deal_wh(0)
        deal_sc(0)
        for a in range(PASSES):
            cast_x(0, a)
            quantize_x(0, a)
            matmuls(0, a, 0)
        nc.vector.tensor_scalar(out=half_bias[:], in0=bias[:], scalar1=0.5, scalar2=None, op0=ALU.mult)
        deal_wh(1)
        deal_sc(1)
        for a in range(PASSES):
            matmuls(0, a, 1)
        cast_x(1, 0)
        multiply(1, 0)
        late = n_tiles - SCALAR_TAIL
        for i in range(n_tiles - 1):
            activate(i, 0)
            blend(i, 0, 0)
            if i - 1 < late:
                cast_out(i - 1)
            cast_x(i + 1, 1)
            blend(i, 0, 1)
            multiply(i + 1, 1)
            cast_x(i + 1, 2)
            blend(i, 0, 2)
            multiply(i + 1, 2)
            if i - 1 < late:
                quantize_out(i - 1)
            activate(i, 1)
            blend(i, 1, 0)
            cast_x(i + 2, 0)
            if i - 1 >= late:
                cast_out(i - 1)
            blend(i, 1, 1)
            multiply(i + 2, 0)
            if i - 1 >= late:
                quantize_out(i - 1)
            blend(i, 1, 2)
        last = n_tiles - 1
        activate(last, 0)
        activate(last, 1)
        cast_out(last - 1)
        for step in range(3):
            blend(last, 0, step)
            blend(last, 1, step)
        quantize_out(last - 1)
        cast_out(last)
        quantize_out(last)

        for q in range(QUADS):
            queue = nc.sync if q % 2 == 0 else nc.scalar
            queue.dma_start(
                out=out_2[0].bitcast(I32)[4 * q : 4 * q + 4, :],
                in_=out_scales[:].bitcast(I32)[32 * q : 32 * q + 4, :],
            )
